import numpy as np
import ml_dtypes


def mxq(x, axis, fmt="e4m3"):
    dtype, down = {"e4m3": (ml_dtypes.float8_e4m3fn, 7), "e5m2": (ml_dtypes.float8_e5m2, 14)}[fmt]
    v = np.moveaxis(np.asarray(x, np.float32).astype(ml_dtypes.bfloat16).astype(np.float64), axis, -1)
    blocks = v.reshape(v.shape[:-1] + (-1, 32))
    amax = np.abs(blocks).max(-1, keepdims=True)
    byte = np.maximum(np.where(amax > 0, np.frexp(amax)[1] - 1 + 127, 0) - down, 1)
    scale = np.exp2(byte - 127.0)
    codes = (blocks / scale).astype(np.float32).astype(dtype).astype(np.float64)
    return np.moveaxis((codes * scale).reshape(v.shape), -1, axis)


WIDE = False


def mx_kscale(k):
    if not WIDE:
        return np.ones(k)
    levels = np.array([10, -10, 5, -5, 0])
    if k % 512:
        return np.exp2(np.random.permutation(np.resize(levels, k // 32))).repeat(32)
    a = np.empty((k // 512, 16))
    for p in range(k // 512):
        a[p, :8] = np.random.permutation(np.resize(levels, 8))
        for g in range(8):
            far = levels[np.abs(levels - a[p, g]) >= 10]
            a[p, g + 8] = far[np.random.randint(len(far))]
    return np.exp2(a.ravel()).repeat(32)


def f64(x):
    return np.asarray(x).astype(np.float64)


def striped8(idx):
    return np.asarray(idx).reshape(8, -1, 16).transpose(0, 2, 1).reshape(128, -1).astype(np.uint16)


def unstriped8(offs):
    return offs.reshape(8, 16, -1).transpose(0, 2, 1).reshape(8, -1).astype(np.int64)


def pick8(x, idx, run):
    r = np.arange(len(x))
    return x[r[:, None], idx[r % (8 * run) // run]]


def bf(x):
    return np.asarray(x, np.float32).astype(ml_dtypes.bfloat16)


def planes(Y):
    r, m = Y.shape
    b = f64(bf(Y)).reshape(r // 32, 32, m)
    amax = np.abs(b).max(1)
    byte = np.clip(np.where(amax > 0, np.frexp(amax)[1] - 1 + 127 - 7, 1), 1, 254)
    codes = (b * np.exp2(127.0 - byte)[:, None, :]).reshape(r, m).astype(np.float32).astype(ml_dtypes.float8_e4m3fn).view(np.uint8)
    words = codes.reshape(r // 512, 128, 4, m).transpose(0, 1, 3, 2)
    return np.ascontiguousarray(words), np.ascontiguousarray(byte.astype(np.uint8).reshape(r // 512, 16, m))


D, T, I, Q, X, E = 512, 2048, 512, 512, 64, 512


def setup_inputs():
    n = np.random.standard_normal
    idx = np.stack([np.random.permutation(T)[:I] for _ in range(8)])
    fd = mx_kscale(D)
    fi = mx_kscale(I)
    ti = np.ones((8, T))
    np.put_along_axis(ti, idx, np.tile(fi, (8, 1)), axis=1)
    return {
        "query": (n((D, Q)) * (np.arange(D)[:, None] // 64 == np.arange(Q) % 8) * 0.0625 * fd[:, None]).astype(np.float32),
        "keys": (n((D, T)) / fd[:, None]).astype(np.float32),
        "size": (np.random.uniform(0.5, 2.0, (1, I)) * fi).astype(np.float32),
        "vals": (n((E, T)) / ti[np.arange(E) % 512 // 64]).astype(np.float32),
        "own": ((np.arange(E)[:, None] // 64 == np.arange(Q) % 8) * 1.0).astype(np.float32),
        "offs": striped8(idx),
    }


def reference(query, keys, size, vals, own, offs):
    idx = unstriped8(offs)
    queryq = mxq(f64(query), 0, "e4m3")
    keysidxq = mxq(pick8(f64(keys), idx, 64), 0, "e4m3")
    a = queryq.T @ keysidxq
    p = np.exp(a - np.max(a, axis=1, keepdims=True))
    w = p * f64(size) / np.sum(p, axis=1, keepdims=True)
    wt = w.T
    vt = pick8(f64(vals), idx, 64).T
    vtq = mxq(vt, 0, "e4m3")
    wtq = mxq(wt, 0, "e4m3")
    o = vtq.T @ wtq
    ob = o * f64(own)
    y = ob.reshape(E, X, Q // X).sum(axis=2)
    words, scales = planes(y)
    return y, words, scales

@@ -1,0 +1,224 @@
+from contextlib import ExitStack
+
+import concourse.mybir as mybir
+from concourse.masks import make_identity
+
+D, T, I, Q, X, E = 512, 2048, 512, 512, 64, 512
+FLOPS = 2 * D * Q * I + 2 * I * E * Q
+
+F32 = mybir.dt.float32
+BF16 = mybir.dt.bfloat16
+I32 = mybir.dt.int32
+U32 = mybir.dt.uint32
+U16 = mybir.dt.uint16
+U8 = mybir.dt.uint8
+FP8X4 = mybir.dt.float8_e4m3fn_x4
+ALU = mybir.AluOpType
+ACT = mybir.ActivationFunctionType
+AX = mybir.AxisListType
+
+P = 128
+PACK = 4
+HEADS = 8
+
+
+def tile_attend_ownlists_heads_pl_kernel(tc, query, keys, size, vals, own, offs, out_0, out_1, out_2):
+    nc = tc.nc
+    with ExitStack() as ctx:
+        sb = ctx.enter_context(tc.tile_pool(name="sb", bufs=1))
+        big = ctx.enter_context(tc.psum_pool(name="big", bufs=4))
+        turn = ctx.enter_context(tc.psum_pool(name="turn", bufs=2))
+
+        def tile(shape, dtype, name):
+            return sb.tile(shape, dtype, name=name, align_bytes=64)
+
+        def quantize(codes, scales, grouped):
+            nc.vector.quantize_mx(out=codes.bitcast(FP8X4), scales=scales, in_=grouped)
+
+        offsets = tile([P, I // 16], U16, "offsets")
+        size_col = tile([P, PACK], F32, "size_col")
+        nc.scalar.dma_start(size_col[:], size.rearrange("o (s t) -> (o s) t", t=PACK))
+
+        key_rows = keys.rearrange("(p t) n -> p t n", t=PACK)
+        key_pool = [tile([P, T], F32, "key_pool%d" % t) for t in range(PACK)]
+        for t in range(PACK):
+            nc.sync.dma_start(key_pool[t][:], key_rows[:, t, :])
+            if t == 0:
+                nc.sync.dma_start(offsets[:], offs)
+        query_rows = query.rearrange("(p t) q -> p t q", t=PACK)
+        half = Q // 2
+        query_raw = [tile([P, PACK, half], F32, "query_raw%d" % h) for h in range(2)]
+        for h in range(2):
+            nc.sync.dma_start(query_raw[h][:], query_rows[:, :, h * half : (h + 1) * half])
+        val_rows = vals.rearrange("(p r) n -> p r n", r=PACK)
+        val_pool = [tile([P, T], F32, "val_pool%d" % r) for r in range(PACK)]
+        for r in range(PACK):
+            nc.sync.dma_start(val_pool[r][:], val_rows[:, r, :])
+        own_rows = own.rearrange("(p r) q -> p r q", r=PACK)
+        own_sb = [tile([P, Q], F32, "own_sb%d" % r) for r in range(PACK)]
+        for r in range(PACK):
+            nc.sync.dma_start(own_sb[r][:], own_rows[:, r, :])
+
+        ident = tile([P, P], F32, "ident")
+        make_identity(nc, ident[:])
+
+        size_ps = turn.tile([P, PACK, P], F32, name="wturn")
+        for t in range(PACK):
+            nc.tensor.transpose(size_ps[:, t, :], size_col[:, t : t + 1].to_broadcast([P, P]), ident[:])
+        size_all = tile([P, I], F32, "size_all")
+        nc.scalar.copy(
+            size_all[:].rearrange("p (u s e) -> p u s e", u=2, e=2),
+            size_ps[:].rearrange("p (u e) s -> p u s e", u=2),
+        )
+
+        key_got = tile([P, PACK, I], BF16, "key_got")
+        key_grp = tile([P, I, PACK], BF16, "key_grp")
+        for pair in range(2):
+            planes = slice(2 * pair, 2 * pair + 2)
+            for t in range(2 * pair, 2 * pair + 2):
+                nc.vector.tensor_copy(key_got[:, t, :], key_pool[t][:].indirect(offsets[:]))
+            nc.vector.tensor_copy(
+                key_grp[:, :, planes].rearrange("p (u s e) t -> p s u e t", u=2, e=2),
+                key_got[:, planes, :].rearrange("p t (s u e) -> p s u e t", u=2, e=2),
+            )
+        key_codes = tile([P, I], U32, "key_codes")
+        key_scales = tile([P, I], U8, "key_scales")
+        quantize(key_codes[:], key_scales[:], key_grp[:].rearrange("p c t -> p (c t)"))
+
+        query_codes = []
+        query_scales = []
+        for h in range(2):
+            grp = tile([P, half, PACK], BF16, "query_grp%d" % h)
+            nc.scalar.copy(
+                grp[:].rearrange("p (c i) t -> p c t i", i=4),
+                query_raw[h][:].rearrange("p t (c i) -> p c t i", i=4),
+            )
+            query_codes.append(tile([P, half], U32, "query_codes%d" % h))
+            query_scales.append(tile([P, half], U8, "query_scales%d" % h))
+            quantize(query_codes[h][:], query_scales[h][:], grp[:].rearrange("p c t -> p (c t)"))
+
+        w_codes = tile([P, Q], U32, "w_codes")
+        w_scales = tile([P, Q], U8, "w_scales")
+        for j in range(Q // P):
+            h, c = divmod(j, 2)
+            cols = slice(c * P, (c + 1) * P)
+            score = big.tile([P, I], F32, name="acc")
+            nc.tensor.matmul_mx(
+                out=score[:],
+                lhsT=query_codes[h][:, cols].bitcast(FP8X4),
+                lhsT_scale=query_scales[h][:, cols],
+                rhs=key_codes[:].bitcast(FP8X4),
+                rhs_scale=key_scales[:],
+                start=True,
+                stop=True,
+            )
+            neg_max = tile([P, 1], F32, "neg_max%d" % j)
+            nc.vector.tensor_reduce(neg_max[:], score[:], AX.X, ALU.max, negate=True)
+            prob = tile([P, I], F32, "prob%d" % j)
+            total = tile([P, 1], F32, "total%d" % j)
+            nc.scalar.activation(prob[:], score[:], ACT.Exp, bias=neg_max[:], scale=1.0, accum_out=total[:])
+            inv = tile([P, 1], F32, "inv%d" % j)
+            nc.vector.reciprocal(inv[:], total[:])
+            weight = tile([P, I], BF16, "weight%d" % j)
+            nc.vector.scalar_tensor_tensor(weight[:], prob[:], inv[:], size_all[:], ALU.mult, ALU.mult)
+            words = weight[:].bitcast(F32)
+            w_ps = turn.tile([P, 2, P], F32, name="wturn")
+            for u in range(2):
+                nc.tensor.transpose(w_ps[:, u, :], words[:, u * P : (u + 1) * P], ident[:])
+            w_grp = tile([P, P * PACK], BF16, "w_grp%d" % j)
+            nc.scalar.copy(
+                w_grp[:].bitcast(F32).rearrange("p (q u) -> p q u", u=2),
+                w_ps[:].rearrange("p u q -> p q u"),
+            )
+            qcols = slice(j * P, (j + 1) * P)
+            quantize(w_codes[:, qcols], w_scales[:, qcols], w_grp[:])
+
+        def gather_and_turn(r):
+            got = tile([P, I], BF16, "val_got%d" % r)
+            if r == 0:
+                cast = tile([P, T], BF16, "val_cast")
+                for c0 in range(0, T, 512):
+                    nc.scalar.activation(cast[:, c0 : c0 + 512], val_pool[r][:, c0 : c0 + 512], ACT.Copy)
+                nc.scalar.activation(got[:], cast[:].indirect(offsets[:]), ACT.Copy)
+            else:
+                nc.vector.tensor_copy(got[:], val_pool[r][:].indirect(offsets[:]))
+            words = got[:].bitcast(F32)
+            v_ps = turn.tile([P, 2, P], F32, name="vturn")
+            for u in range(2):
+                nc.tensor.transpose(v_ps[:, u, :], words[:, u : I // 2 : 2], ident[:])
+            v_grp = tile([P, P * PACK], BF16, "v_grp%d" % r)
+            nc.scalar.copy(
+                v_grp[:].bitcast(F32).rearrange("p (c u) -> p c u", u=2),
+                v_ps[:].rearrange("p u c -> p c u"),
+            )
+            return v_grp
+
+        def multiply(r, v_grp):
+            v_codes = tile([P, P], U32, "v_codes%d" % r)
+            v_scales = tile([P, P], U8, "v_scales%d" % r)
+            quantize(v_codes[:], v_scales[:], v_grp[:])
+            parts = []
+            width = half if r == PACK - 1 else Q
+            for c0 in range(0, Q, width):
+                cols = slice(c0, c0 + width)
+                if c0:
+                    acc = turn.tile([P, width], F32, name="wturn")
+                else:
+                    acc = big.tile([P, width], F32, name="acc")
+                nc.tensor.matmul_mx(
+                    out=acc[:],
+                    lhsT=v_codes[:].bitcast(FP8X4),
+                    lhsT_scale=v_scales[:],
+                    rhs=w_codes[:, cols].bitcast(FP8X4),
+                    rhs_scale=w_scales[:, cols],
+                    start=True,
+                    stop=True,
+                )
+                parts.append((cols, acc))
+            return parts
+
+        grp = [gather_and_turn(r) for r in range(3)]
+        accs = [multiply(r, grp[r]) for r in range(2)]
+        grp.append(gather_and_turn(3))
+        accs.extend(multiply(r, grp[r]) for r in range(2, PACK))
+
+        y = tile([P, PACK, X], F32, "y")
+        later = []
+        for r in range(PACK):
+            for cols, acc in accs[r]:
+                masked = tile([P, cols.stop - cols.start], F32, "masked%d_%d" % (r, cols.start))
+                if r < 2:
+                    nc.vector.tensor_tensor(
+                        masked[:].rearrange("p (g x h) -> p x g h", g=2, h=4),
+                        acc[:].rearrange("p (x g h) -> p x g h", g=2, h=4),
+                        own_sb[r][:].rearrange("p (x g h) -> p x g h", g=2, h=4),
+                        ALU.mult,
+                    )
+                    four = tile([P, X, 4], F32, "four%d" % r)
+                    nc.gpsimd.tensor_tensor(
+                        four[:].rearrange("p x h -> p (x h)"), masked[:, :half], masked[:, half:], ALU.add
+                    )
+                    two = tile([P, X, 2], F32, "two%d" % r)
+                    nc.gpsimd.tensor_tensor(two[:], four[:, :, 0:2], four[:, :, 2:4], ALU.add)
+                    nc.gpsimd.tensor_tensor(y[:, r, :], two[:, :, 0], two[:, :, 1], ALU.add)
+                else:
+                    nc.vector.tensor_tensor(masked[:], acc[:], own_sb[r][:, cols], ALU.mult)
+                    later.append((r, cols, masked))
+        for r, cols, masked in later:
+            nc.vector.tensor_reduce(
+                y[:, r, cols.start // HEADS : cols.stop // HEADS],
+                masked[:].rearrange("p (x h) -> p x h", h=HEADS),
+                AX.X,
+                ALU.add,
+            )
+
+        nc.sync.dma_start(out_0.rearrange("(p r) x -> p r x", r=PACK), y[:])
+        y_grp = tile([P, X, PACK], BF16, "y_grp")
+        nc.vector.tensor_copy(y_grp[:], y[:].rearrange("p r x -> p x r"))
+        y_codes = tile([P, X], U32, "y_codes")
+        y_scales = tile([P, X], U8, "y_scales")
+        quantize(y_codes[:], y_scales[:], y_grp[:].rearrange("p x r -> p (x r)"))
+        nc.sync.dma_start(out_1[0].rearrange("p c r -> p (c r)").bitcast(I32), y_codes[:].bitcast(I32))
+        for g in range(4):
+            queue = nc.scalar if g % 2 else nc.sync
+            queue.dma_start(out_2[0, 4 * g : 4 * g + 4, :].bitcast(I32), y_scales[32 * g : 32 * g + 4, :].bitcast(I32))

@@ -51,8 +51,11 @@ def tile_attend_ownlists_heads_pl_kernel(tc, query, keys, size, vals, own, offs,
         for h in range(2):
             nc.sync.dma_start(query_raw[h][:], query_rows[:, :, h * half : (h + 1) * half])
         val_rows = vals.rearrange("(p r) n -> p r n", r=PACK)
-        val_pool = [tile([P, T], F32, "val_pool%d" % r) for r in range(PACK)]
-        for r in range(PACK):
+        val_half = [tile([P, T // 2], F32, "val_half%d" % h) for h in range(2)]
+        for h in range(2):
+            nc.sync.dma_start(val_half[h][:], val_rows[:, 0, h * T // 2 : (h + 1) * T // 2])
+        val_pool = [None] + [tile([P, T], F32, "val_pool%d" % r) for r in range(1, PACK)]
+        for r in range(1, PACK):
             nc.sync.dma_start(val_pool[r][:], val_rows[:, r, :])
         own_rows = own.rearrange("(p r) q -> p r q", r=PACK)
         own_sb = [tile([P, Q], F32, "own_sb%d" % r) for r in range(PACK)]
@@ -97,6 +100,12 @@ def tile_attend_ownlists_heads_pl_kernel(tc, query, keys, size, vals, own, offs,
             query_scales.append(tile([P, half], U8, "query_scales%d" % h))
             quantize(query_codes[h][:], query_scales[h][:], grp[:].rearrange("p c t -> p (c t)"))
 
+        cast = tile([P, T], BF16, "val_cast")
+        for h in range(2):
+            nc.scalar.activation(cast[:, h * T // 2 : (h + 1) * T // 2], val_half[h][:], ACT.Copy)
+
+        neg_max = tile([P, Q // P], F32, "query_grp1")
+        total = tile([P, Q // P], F32, "val_half1")
         w_codes = tile([P, Q], U32, "w_codes")
         w_scales = tile([P, Q], U8, "w_scales")
         for j in range(Q // P):
@@ -112,13 +121,11 @@ def tile_attend_ownlists_heads_pl_kernel(tc, query, keys, size, vals, own, offs,
                 start=True,
                 stop=True,
             )
-            neg_max = tile([P, 1], F32, "neg_max%d" % j)
-            nc.vector.tensor_reduce(neg_max[:], score[:], AX.X, ALU.max, negate=True)
+            nc.vector.tensor_reduce(neg_max[:, j : j + 1], score[:], AX.X, ALU.max, negate=True)
             prob = tile([P, I], F32, "prob%d" % j)
-            total = tile([P, 1], F32, "total%d" % j)
-            nc.scalar.activation(prob[:], score[:], ACT.Exp, bias=neg_max[:], scale=1.0, accum_out=total[:])
+            nc.scalar.activation(prob[:], score[:], ACT.Exp, bias=neg_max[:, j : j + 1], scale=1.0, accum_out=total[:, j : j + 1])
             inv = tile([P, 1], F32, "inv%d" % j)
-            nc.vector.reciprocal(inv[:], total[:])
+            nc.vector.reciprocal(inv[:], total[:, j : j + 1])
             weight = tile([P, I], BF16, "weight%d" % j)
             nc.vector.scalar_tensor_tensor(weight[:], prob[:], inv[:], size_all[:], ALU.mult, ALU.mult)
             words = weight[:].bitcast(F32)
@@ -136,9 +143,6 @@ def tile_attend_ownlists_heads_pl_kernel(tc, query, keys, size, vals, own, offs,
         def gather_and_turn(r):
             got = tile([P, I], BF16, "val_got%d" % r)
             if r == 0:
-                cast = tile([P, T], BF16, "val_cast")
-                for c0 in range(0, T, 512):
-                    nc.scalar.activation(cast[:, c0 : c0 + 512], val_pool[r][:, c0 : c0 + 512], ACT.Copy)
                 nc.scalar.activation(got[:], cast[:].indirect(offsets[:]), ACT.Copy)
             else:
                 nc.vector.tensor_copy(got[:], val_pool[r][:].indirect(offsets[:]))
@@ -154,7 +158,7 @@ def tile_attend_ownlists_heads_pl_kernel(tc, query, keys, size, vals, own, offs,
             return v_grp
 
         def multiply(r, v_grp):
-            v_codes = tile([P, P], U32, "v_codes%d" % r)
+            v_codes = tile([P, P], U32, "val_pool3" if r == 2 else "v_codes%d" % r)
             v_scales = tile([P, P], U8, "v_scales%d" % r)
             quantize(v_codes[:], v_scales[:], v_grp[:])
             parts = []

from contextlib import ExitStack

import concourse.mybir as mybir
from concourse.masks import make_identity

D, T, I, Q, X, E = 512, 2048, 512, 512, 64, 512
FLOPS = 2 * D * Q * I + 2 * I * E * Q

F32 = mybir.dt.float32
BF16 = mybir.dt.bfloat16
I32 = mybir.dt.int32
U32 = mybir.dt.uint32
U16 = mybir.dt.uint16
U8 = mybir.dt.uint8
FP8X4 = mybir.dt.float8_e4m3fn_x4
ALU = mybir.AluOpType
ACT = mybir.ActivationFunctionType
AX = mybir.AxisListType

P = 128
PACK = 4
HEADS = 8


def tile_attend_ownlists_heads_pl_kernel(tc, query, keys, size, vals, own, offs, out_0, out_1, out_2):
    nc = tc.nc
    with ExitStack() as ctx:
        sb = ctx.enter_context(tc.tile_pool(name="sb", bufs=1))
        big = ctx.enter_context(tc.psum_pool(name="big", bufs=4))
        turn = ctx.enter_context(tc.psum_pool(name="turn", bufs=2))

        def tile(shape, dtype, name):
            return sb.tile(shape, dtype, name=name, align_bytes=64)

        def quantize(codes, scales, grouped):
            nc.vector.quantize_mx(out=codes.bitcast(FP8X4), scales=scales, in_=grouped)

        offsets = tile([P, I // 16], U16, "offsets")
        size_col = tile([P, PACK], F32, "size_col")
        nc.scalar.dma_start(size_col[:], size.rearrange("o (s t) -> (o s) t", t=PACK))

        key_rows = keys.rearrange("(p t) n -> p t n", t=PACK)
        key_pool = [tile([P, T], F32, "key_pool%d" % t) for t in range(PACK)]
        for t in range(PACK):
            nc.sync.dma_start(key_pool[t][:], key_rows[:, t, :])
            if t == 0:
                nc.sync.dma_start(offsets[:], offs)
        query_rows = query.rearrange("(p t) q -> p t q", t=PACK)
        half = Q // 2
        query_raw = [tile([P, PACK, half], F32, "query_raw%d" % h) for h in range(2)]
        for h in range(2):
            nc.sync.dma_start(query_raw[h][:], query_rows[:, :, h * half : (h + 1) * half])
        val_rows = vals.rearrange("(p r) n -> p r n", r=PACK)
        val_half = [tile([P, T // 2], F32, "val_half%d" % h) for h in range(2)]
        for h in range(2):
            nc.sync.dma_start(val_half[h][:], val_rows[:, 0, h * T // 2 : (h + 1) * T // 2])
        val_pool = [None] + [tile([P, T], F32, "val_pool%d" % r) for r in range(1, PACK)]
        for r in range(1, PACK):
            nc.sync.dma_start(val_pool[r][:], val_rows[:, r, :])
        own_rows = own.rearrange("(p r) q -> p r q", r=PACK)
        own_sb = [tile([P, Q], F32, "own_sb%d" % r) for r in range(PACK)]
        for r in range(PACK):
            nc.sync.dma_start(own_sb[r][:], own_rows[:, r, :])

        ident = tile([P, P], F32, "ident")
        make_identity(nc, ident[:])

        size_ps = turn.tile([P, PACK, P], F32, name="wturn")
        for t in range(PACK):
            nc.tensor.transpose(size_ps[:, t, :], size_col[:, t : t + 1].to_broadcast([P, P]), ident[:])
        size_all = tile([P, I], F32, "size_all")
        nc.scalar.copy(
            size_all[:].rearrange("p (u s e) -> p u s e", u=2, e=2),
            size_ps[:].rearrange("p (u e) s -> p u s e", u=2),
        )

        key_got = tile([P, PACK, I], BF16, "key_got")
        key_grp = tile([P, I, PACK], BF16, "key_grp")
        for pair in range(2):
            planes = slice(2 * pair, 2 * pair + 2)
            for t in range(2 * pair, 2 * pair + 2):
                nc.vector.tensor_copy(key_got[:, t, :], key_pool[t][:].indirect(offsets[:]))
            nc.vector.tensor_copy(
                key_grp[:, :, planes].rearrange("p (u s e) t -> p s u e t", u=2, e=2),
                key_got[:, planes, :].rearrange("p t (s u e) -> p s u e t", u=2, e=2),
            )
        key_codes = tile([P, I], U32, "key_codes")
        key_scales = tile([P, I], U8, "key_scales")
        quantize(key_codes[:], key_scales[:], key_grp[:].rearrange("p c t -> p (c t)"))

        query_codes = []
        query_scales = []
        for h in range(2):
            grp = tile([P, half, PACK], BF16, "query_grp%d" % h)
            nc.scalar.copy(
                grp[:].rearrange("p (c i) t -> p c t i", i=4),
                query_raw[h][:].rearrange("p t (c i) -> p c t i", i=4),
            )
            query_codes.append(tile([P, half], U32, "query_codes%d" % h))
            query_scales.append(tile([P, half], U8, "query_scales%d" % h))
            quantize(query_codes[h][:], query_scales[h][:], grp[:].rearrange("p c t -> p (c t)"))

        cast = tile([P, T], BF16, "val_cast")
        for h in range(2):
            nc.scalar.activation(cast[:, h * T // 2 : (h + 1) * T // 2], val_half[h][:], ACT.Copy)

        neg_max = tile([P, Q // P], F32, "query_grp1")
        total = tile([P, Q // P], F32, "val_half1")
        w_codes = tile([P, Q], U32, "w_codes")
        w_scales = tile([P, Q], U8, "w_scales")
        for j in range(Q // P):
            h, c = divmod(j, 2)
            cols = slice(c * P, (c + 1) * P)
            score = big.tile([P, I], F32, name="acc")
            nc.tensor.matmul_mx(
                out=score[:],
                lhsT=query_codes[h][:, cols].bitcast(FP8X4),
                lhsT_scale=query_scales[h][:, cols],
                rhs=key_codes[:].bitcast(FP8X4),
                rhs_scale=key_scales[:],
                start=True,
                stop=True,
            )
            nc.vector.tensor_reduce(neg_max[:, j : j + 1], score[:], AX.X, ALU.max, negate=True)
            prob = tile([P, I], F32, "prob%d" % j)
            nc.scalar.activation(prob[:], score[:], ACT.Exp, bias=neg_max[:, j : j + 1], scale=1.0, accum_out=total[:, j : j + 1])
            inv = tile([P, 1], F32, "inv%d" % j)
            nc.vector.reciprocal(inv[:], total[:, j : j + 1])
            weight = tile([P, I], BF16, "weight%d" % j)
            nc.vector.scalar_tensor_tensor(weight[:], prob[:], inv[:], size_all[:], ALU.mult, ALU.mult)
            words = weight[:].bitcast(F32)
            w_ps = turn.tile([P, 2, P], F32, name="wturn")
            for u in range(2):
                nc.tensor.transpose(w_ps[:, u, :], words[:, u * P : (u + 1) * P], ident[:])
            w_grp = tile([P, P * PACK], BF16, "w_grp%d" % j)
            nc.scalar.copy(
                w_grp[:].bitcast(F32).rearrange("p (q u) -> p q u", u=2),
                w_ps[:].rearrange("p u q -> p q u"),
            )
            qcols = slice(j * P, (j + 1) * P)
            quantize(w_codes[:, qcols], w_scales[:, qcols], w_grp[:])

        def gather_and_turn(r):
            got = tile([P, I], BF16, "val_got%d" % r)
            if r == 0:
                nc.scalar.activation(got[:], cast[:].indirect(offsets[:]), ACT.Copy)
            else:
                nc.vector.tensor_copy(got[:], val_pool[r][:].indirect(offsets[:]))
            words = got[:].bitcast(F32)
            v_ps = turn.tile([P, 2, P], F32, name="vturn")
            for u in range(2):
                nc.tensor.transpose(v_ps[:, u, :], words[:, u : I // 2 : 2], ident[:])
            v_grp = tile([P, P * PACK], BF16, "v_grp%d" % r)
            nc.scalar.copy(
                v_grp[:].bitcast(F32).rearrange("p (c u) -> p c u", u=2),
                v_ps[:].rearrange("p u c -> p c u"),
            )
            return v_grp

        def multiply(r, v_grp):
            v_codes = tile([P, P], U32, "val_pool3" if r == 2 else "v_codes%d" % r)
            v_scales = tile([P, P], U8, "v_scales%d" % r)
            quantize(v_codes[:], v_scales[:], v_grp[:])
            parts = []
            width = half if r == PACK - 1 else Q
            for c0 in range(0, Q, width):
                cols = slice(c0, c0 + width)
                if c0:
                    acc = turn.tile([P, width], F32, name="wturn")
                else:
                    acc = big.tile([P, width], F32, name="acc")
                nc.tensor.matmul_mx(
                    out=acc[:],
                    lhsT=v_codes[:].bitcast(FP8X4),
                    lhsT_scale=v_scales[:],
                    rhs=w_codes[:, cols].bitcast(FP8X4),
                    rhs_scale=w_scales[:, cols],
                    start=True,
                    stop=True,
                )
                parts.append((cols, acc))
            return parts

        grp = [gather_and_turn(r) for r in range(3)]
        accs = [multiply(r, grp[r]) for r in range(2)]
        grp.append(gather_and_turn(3))
        accs.extend(multiply(r, grp[r]) for r in range(2, PACK))

        y = tile([P, PACK, X], F32, "y")
        later = []
        for r in range(PACK):
            for cols, acc in accs[r]:
                masked = tile([P, cols.stop - cols.start], F32, "masked%d_%d" % (r, cols.start))
                if r < 2:
                    nc.vector.tensor_tensor(
                        masked[:].rearrange("p (g x h) -> p x g h", g=2, h=4),
                        acc[:].rearrange("p (x g h) -> p x g h", g=2, h=4),
                        own_sb[r][:].rearrange("p (x g h) -> p x g h", g=2, h=4),
                        ALU.mult,
                    )
                    four = tile([P, X, 4], F32, "four%d" % r)
                    nc.gpsimd.tensor_tensor(
                        four[:].rearrange("p x h -> p (x h)"), masked[:, :half], masked[:, half:], ALU.add
                    )
                    two = tile([P, X, 2], F32, "two%d" % r)
                    nc.gpsimd.tensor_tensor(two[:], four[:, :, 0:2], four[:, :, 2:4], ALU.add)
                    nc.gpsimd.tensor_tensor(y[:, r, :], two[:, :, 0], two[:, :, 1], ALU.add)
                else:
                    nc.vector.tensor_tensor(masked[:], acc[:], own_sb[r][:, cols], ALU.mult)
                    later.append((r, cols, masked))
        for r, cols, masked in later:
            nc.vector.tensor_reduce(
                y[:, r, cols.start // HEADS : cols.stop // HEADS],
                masked[:].rearrange("p (x h) -> p x h", h=HEADS),
                AX.X,
                ALU.add,
            )

        nc.sync.dma_start(out_0.rearrange("(p r) x -> p r x", r=PACK), y[:])
        y_grp = tile([P, X, PACK], BF16, "y_grp")
        nc.vector.tensor_copy(y_grp[:], y[:].rearrange("p r x -> p x r"))
        y_codes = tile([P, X], U32, "y_codes")
        y_scales = tile([P, X], U8, "y_scales")
        quantize(y_codes[:], y_scales[:], y_grp[:].rearrange("p x r -> p (x r)"))
        nc.sync.dma_start(out_1[0].rearrange("p c r -> p (c r)").bitcast(I32), y_codes[:].bitcast(I32))
        for g in range(4):
            queue = nc.scalar if g % 2 else nc.sync
            queue.dma_start(out_2[0, 4 * g : 4 * g + 4, :].bitcast(I32), y_scales[32 * g : 32 * g + 4, :].bitcast(I32))
